import numpy as np
import ml_dtypes


def mxq(x, axis, fmt="e4m3"):
    dtype, down = {"e4m3": (ml_dtypes.float8_e4m3fn, 7), "e5m2": (ml_dtypes.float8_e5m2, 14)}[fmt]
    v = np.moveaxis(np.asarray(x, np.float32).astype(ml_dtypes.bfloat16).astype(np.float64), axis, -1)
    blocks = v.reshape(v.shape[:-1] + (-1, 32))
    amax = np.abs(blocks).max(-1, keepdims=True)
    byte = np.maximum(np.where(amax > 0, np.frexp(amax)[1] - 1 + 127, 0) - down, 1)
    scale = np.exp2(byte - 127.0)
    codes = (blocks / scale).astype(np.float32).astype(dtype).astype(np.float64)
    return np.moveaxis((codes * scale).reshape(v.shape), -1, axis)


WIDE = False


def mx_kscale(k):
    if not WIDE:
        return np.ones(k)
    levels = np.array([10, -10, 5, -5, 0])
    if k % 512:
        return np.exp2(np.random.permutation(np.resize(levels, k // 32))).repeat(32)
    a = np.empty((k // 512, 16))
    for p in range(k // 512):
        a[p, :8] = np.random.permutation(np.resize(levels, 8))
        for g in range(8):
            far = levels[np.abs(levels - a[p, g]) >= 10]
            a[p, g + 8] = far[np.random.randint(len(far))]
    return np.exp2(a.ravel()).repeat(32)


def f64(x):
    return np.asarray(x).astype(np.float64)


def striped(idx):
    return np.tile(idx.reshape(-1, 16).T, (8, 1)).astype(np.uint16)


def unstriped(offs):
    return offs[:16].T.reshape(-1).astype(np.int64)


E2M1 = np.array([0.0, 0.5, 1.0, 1.5, 2.0, 3.0, 4.0, 6.0, -0.0, -0.5, -1.0, -1.5, -2.0, -3.0, -4.0, -6.0])


def pack_weight(w, fmt):
    k, n = w.shape
    w = f64(np.asarray(w, np.float32).astype(ml_dtypes.bfloat16)).reshape(k // 32, 32, n)
    amax = np.abs(w).max(1)
    if fmt == "e4m3":
        byte = np.frexp(amax)[1] - 1 + 127 - 7
    else:
        mant, ex = np.frexp(amax / 6.0)
        byte = np.where(mant > 0.5, ex, ex - 1) + 127
    byte = np.clip(np.where(amax > 0, byte, 1), 1, 254)
    scaled = (w * np.exp2(127.0 - byte)[:, None, :]).reshape(k, n).astype(np.float32)
    by_word = np.ascontiguousarray(scaled.reshape(k // 512, 128, 4, n).transpose(0, 1, 3, 2))
    if fmt == "e4m3":
        words = by_word.astype(ml_dtypes.float8_e4m3fn).view(np.uint8)
    else:
        c = by_word.astype(ml_dtypes.float4_e2m1fn).view(np.uint8) & 0xF
        words = (c[..., 0::2] | (c[..., 1::2] << 4)).reshape(k // 512, 128, 2 * n)
    return np.ascontiguousarray(words), np.ascontiguousarray(byte.astype(np.uint8).reshape(k // 512, 16, n))


def unpack_weight(words, scales, fmt):
    g, _, n = scales.shape
    words = np.ascontiguousarray(words).reshape(g, 128, n, -1)
    if fmt == "e4m3":
        vals = words.view(ml_dtypes.float8_e4m3fn).astype(np.float64)
    else:
        nib = np.empty((g, 128, n, 4), np.uint8)
        nib[..., 0::2] = words & 0xF
        nib[..., 1::2] = words >> 4
        vals = E2M1[nib]
    vals = vals * np.repeat(np.exp2(scales.astype(np.float64) - 127.0), 8, axis=1)[..., None]
    return vals.transpose(0, 1, 3, 2).reshape(g * 512, n)


def gelu(v):
    return 0.5 * v * (1.0 + np.tanh(np.sqrt(2.0 / np.pi) * (v + 0.044715 * v**3)))


K, H, M, N, T, S, T2, P = 1024, 512, 512, 256, 4096, 1024, 2048, 512

def setup_inputs():
    n = np.random.standard_normal
    s = mx_kscale(K)[:, None]
    u = mx_kscale(H)[:, None]
    d = mx_kscale(M)[:, None]
    perm = np.random.permutation(T2)
    tab_words, tab_scales = pack_weight(n((K, T)) * s, "e4m3")
    w2_words, w2_scales = pack_weight(n((K, H)) / np.sqrt(K) / s, "e2m1")
    w4_words, w4_scales = pack_weight(1.5 * n((M, N)) / np.sqrt(M) / d, "e2m1")
    return {"tab_words": tab_words, "tab_scales": tab_scales,
            "offs": striped(np.random.permutation(T)[:S]),
            "offs2": striped(np.random.permutation(T2)[:S]),
            "offs3": striped(perm[:P]), "offs4": striped(perm[P:2 * P]),
            "w1": (n((K, H)) / np.sqrt(K) / s).astype(np.float32),
            "w2_words": w2_words, "w2_scales": w2_scales,
            "gain": (np.exp(0.4 * n(H)) * u[:, 0]).astype(np.float32),
            "wgs": np.exp(0.3 * n((128, S))).astype(np.float32),
            "page0": (n((H, T2)) * u).astype(np.float32),
            "mix": (0.7 * n(H)).astype(np.float32),
            "w3": (1.2 * n((H, M)) / np.sqrt(H) / u).astype(np.float32),
            "lift": (np.exp(0.4 * n(M)) * d[:, 0]).astype(np.float32),
            "w4_words": w4_words, "w4_scales": w4_scales}

def reference(tab_words, tab_scales, offs, offs2, offs3, offs4, w1, w2_words, w2_scales, gain, wgs, page0, mix, w3, lift, w4_words, w4_scales):
    v = unpack_weight(tab_words, tab_scales, "e4m3")[:, unstriped(offs)]
    w2 = unpack_weight(w2_words, w2_scales, "e2m1")
    w4 = unpack_weight(w4_words, w4_scales, "e2m1")
    p1 = mxq(f64(w1), 0, "e4m3").T @ v
    p2 = w2.T @ v
    h = f64(gain)[:, None] * np.maximum(p1, p2)
    page = f64(page0).copy()
    page[:, unstriped(offs2)] = np.tile(f64(wgs), (H // 128, 1)) * h
    a = page[:, unstriped(offs3)]
    b = page[:, unstriped(offs4)]
    page[:, unstriped(offs3)] = a + f64(mix)[:, None] * b
    page[:, unstriped(offs4)] = np.maximum(a, b)
    y = np.tanh(mxq(f64(w3), 0, "e4m3").T @ mxq(page, 0, "e4m3"))
    z = f64(lift)[:, None] * y
    return w4.T @ mxq(z, 0, "e4m3")

@@ -1,0 +1,322 @@
+from contextlib import ExitStack
+
+import concourse.mybir as mybir
+
+K, H, M, N, T, S, T2, PAIRS = 1024, 512, 512, 256, 4096, 1024, 2048, 512
+FLOPS = 2 * (2 * K * H * S + H * M * T2 + M * N * T2)
+
+F32 = mybir.dt.float32
+BF16 = mybir.dt.bfloat16
+I32 = mybir.dt.int32
+U32 = mybir.dt.uint32
+U16 = mybir.dt.uint16
+U8 = mybir.dt.uint8
+FP8X4 = mybir.dt.float8_e4m3fn_x4
+FP4X4 = mybir.dt.float4_e2m1fn_x4
+ALU = mybir.AluOpType
+ACT = mybir.ActivationFunctionType
+
+P = 128
+PACK = 4
+PASSES = K // (P * PACK)
+HALF = 512
+CHUNK = 256
+WIDTHS = (CHUNK // 2,) + (CHUNK,) * (T2 // CHUNK - 1) + (CHUNK // 2,)
+STARTS = tuple(sum(WIDTHS[:c]) for c in range(len(WIDTHS)))
+CHUNKS = len(WIDTHS)
+SUB = 128
+SLOT_ORDER = (0, 2, 3, 1)
+VECTOR_ROUNDED_CHUNKS = 6
+
+
+def tile_list_cube_cache_scores_kernel(
+    tc, tab_words, tab_scales, offs, offs2, offs3, offs4, w1, w2_words, w2_scales,
+    gain, wgs, page0, mix, w3, lift, w4_words, w4_scales, out,
+):
+    nc = tc.nc
+    with ExitStack() as ctx:
+        keep = ctx.enter_context(tc.tile_pool(name="keep", bufs=1))
+        work = ctx.enter_context(tc.tile_pool(name="work", bufs=2))
+        psum = ctx.enter_context(tc.psum_pool(name="psum", bufs=4))
+
+        def held(name, shape, dtype):
+            return keep.tile(shape, dtype, name=name, align_bytes=64)
+
+        def load_scale_rows(queue, plane, scales):
+            for quad in range(4):
+                queue.dma_start(
+                    out=plane[32 * quad : 32 * quad + 4, :, :].bitcast(I32),
+                    in_=scales[:, 4 * quad : 4 * quad + 4, :].rearrange("a r c -> r a c").bitcast(I32),
+                )
+
+        def load_list(name, src, entries):
+            lst = keep.tile([P, entries // 16], U16, name=name)
+            nc.sync.dma_start(lst[:], src)
+            return lst
+
+        def load_per_row(queue, name, vec):
+            col = held(name, [P, PACK], F32)
+            queue.dma_start(out=col[:], in_=vec.rearrange("(p t) -> p t", t=PACK))
+            return col
+
+        def load_weight(rows):
+            raw = work.tile([P, PACK, H], F32, name="raw", align_bytes=64)
+            nc.sync.dma_start(out=raw[:], in_=rows.rearrange("(p j) c -> p j c", j=PACK))
+            return raw
+
+        def group_weight(name, raw, slots, on_vector):
+            count = slots.stop - slots.start
+            grouped = held(name + "_grouped", [P, count, SUB, PACK], BF16)
+            dst = grouped[:].rearrange("p t m j -> p m t j")
+            src = raw[:].rearrange("p j (m t) -> p m t j", t=PACK)[:, :, slots, :]
+            if on_vector:
+                nc.vector.tensor_copy(out=dst, in_=src)
+            else:
+                nc.scalar.copy(out=dst, in_=src)
+            return grouped
+
+        def quantize_weight(name, grouped, codes_tag):
+            width = grouped.shape[1] * SUB
+            codes = keep.tile([P, width], U32, name=name + "_codes", tag=codes_tag, align_bytes=64)
+            plane = held(name + "_plane", [P, width], U8)
+            nc.vector.quantize_mx(
+                out=codes[:].bitcast(FP8X4), scales=plane[:], in_=grouped[:].rearrange("p t m j -> p (t m j)")
+            )
+            return codes, plane
+
+        tab_rows = held("tab_rows", [P, T], U8)
+        nc.vector.memset(tab_rows[0:96, :].bitcast(I32), 0)
+        w2_plane_raw = held("w2_plane_raw", [P, PASSES, H], U8)
+        nc.gpsimd.memset(w2_plane_raw[:].bitcast(I32), 0)
+        v_plane = [held("v_plane%d" % a, [P, S], U8) for a in range(PASSES)]
+        for a in range(PASSES):
+            nc.gpsimd.memset(v_plane[a][:].bitcast(I32), 0)
+        w4_plane = held("w4_plane", [P, 1, N], U8)
+        nc.gpsimd.memset(w4_plane[:].bitcast(I32), 0)
+
+        list1 = load_list("list1", offs, S)
+        nc.sync.dma_start(
+            out=tab_rows[96:P, :].bitcast(I32), in_=tab_scales.rearrange("a q t -> (a q) t").bitcast(I32)
+        )
+        w2_raw = held("w2_raw", [P, PASSES, 2 * H], U8)
+        nc.sync.dma_start(out=w2_raw[:].bitcast(I32), in_=w2_words.rearrange("a p c -> p a c").bitcast(I32))
+        load_scale_rows(nc.scalar, w2_plane_raw, w2_scales)
+        tab = [held("tab%d" % a, [P, T], I32) for a in range(PASSES)]
+        for a in range(PASSES):
+            nc.sync.dma_start(out=tab[a][:], in_=tab_words[a].rearrange("p t i -> p (t i)").bitcast(I32))
+        w1_raw = [load_weight(w1[a * P * PACK : (a + 1) * P * PACK, :]) for a in range(PASSES)]
+        lead, rest = slice(0, 1), slice(1, PACK)
+        w1_lead = [group_weight("w1_lead0", w1_raw[0], lead, False)]
+
+        wgs_rows = wgs.rearrange("(q t) j -> t q j", t=PACK)
+        page_rows = page0.rearrange("(p t) c -> t p c", t=PACK)
+        factor, page = {}, {}
+
+        def load_factor(t):
+            factor[t] = held("factor%d" % t, [P, S], F32)
+            for quad in (0, 2, 1, 3):
+                nc.sync.dma_start(out=factor[t][32 * quad : 32 * quad + 32, :], in_=wgs_rows[t])
+            nc.scalar.activation(out=factor[t][:], in_=factor[t][:], func=ACT.Copy, scale=gain_col[:, t : t + 1])
+
+        def load_page(t):
+            page[t] = keep.tile([P, T2], F32, name="page%d" % t, tag="page%d" % t)
+            nc.sync.dma_start(out=page[t][:], in_=page_rows[t])
+
+        gain_col = load_per_row(nc.sync, "gain_col", gain)
+        load_factor(SLOT_ORDER[0])
+        load_page(SLOT_ORDER[0])
+        list2 = load_list("list2", offs2, S)
+        list3 = load_list("list3", offs3, PAIRS)
+        list4 = load_list("list4", offs4, PAIRS)
+        mix_col = load_per_row(nc.sync, "mix_col", mix)
+        w1_rest = [group_weight("w1_rest0", w1_raw[0], rest, False)]
+        load_factor(SLOT_ORDER[1])
+        load_factor(SLOT_ORDER[2])
+        load_page(SLOT_ORDER[1])
+
+        picked_rows = held("picked_rows", [P, S], U8)
+        nc.vector.tensor_copy(picked_rows[:], tab_rows[:].indirect(list1[:]))
+        for a in range(PASSES):
+            for quad in range(4):
+                row = 96 + 16 * a + 4 * quad
+                nc.gpsimd.dma_start(
+                    out=v_plane[a][32 * quad : 32 * quad + 4, :].bitcast(I32),
+                    in_=picked_rows[row : row + 4, :].bitcast(I32),
+                )
+
+        v_codes = {}
+
+        def gather_words(a):
+            for h in range(S // HALF):
+                v_codes[a, h] = held("v_codes%d%d" % (a, h), [P, HALF], U32)
+                cols = slice(h * HALF // 16, (h + 1) * HALF // 16)
+                nc.vector.tensor_copy(v_codes[a, h][:], tab[a][:].bitcast(U32).indirect(list1[:, cols]))
+
+        w2_codes = held("w2_codes", [P, PASSES, PACK, 2 * SUB], U8)
+        w2_plane = held("w2_plane", [P, PASSES, PACK, SUB], U8)
+        for a in range(PASSES):
+            nc.vector.tensor_copy(
+                out=w2_codes[:, a].rearrange("p t (m b) -> p t m b", b=2),
+                in_=w2_raw[:, a].rearrange("p (m t b) -> p t m b", t=PACK, b=2),
+            )
+        gather_words(0)
+        nc.vector.tensor_copy(out=w2_plane[:], in_=w2_plane_raw[:].rearrange("p a (m t) -> p a t m", t=PACK))
+        gather_words(1)
+        w1_lead.append(group_weight("w1_lead1", w1_raw[1], lead, True))
+        lead_q = [quantize_weight("w1_lead%d" % a, w1_lead[a], "w1_lead_codes%d" % a) for a in range(PASSES)]
+        w1_rest.append(group_weight("w1_rest1", w1_raw[1], rest, True))
+
+        w3_raw = load_weight(w3)
+        w3_grouped = group_weight("w3", w3_raw, slice(0, PACK), False)
+        load_factor(SLOT_ORDER[3])
+        lift_col = load_per_row(nc.sync, "lift_col", lift)
+        w4_codes = held("w4_codes", [P, 2 * N], U8)
+        nc.sync.dma_start(out=w4_codes[:].bitcast(I32), in_=w4_words[0].bitcast(I32))
+        load_scale_rows(nc.sync, w4_plane, w4_scales)
+
+        larger, mover, opponent, mixed, top = {}, {}, {}, {}, {}
+        first_sum, second_sum = {}, {}
+
+        def products(t):
+            w1_q, place = (lead_q, 0) if t == 0 else (rest_q, t - 1)
+            rows = slice(place * SUB, (place + 1) * SUB)
+            for h in range(S // HALF):
+                cols = slice(h * HALF, (h + 1) * HALF)
+                p2 = psum.tile([P, HALF], F32, name="bank_b")
+                p1 = psum.tile([P, HALF], F32, name="bank_a")
+                for a in range(PASSES):
+                    nc.tensor.matmul_mx(
+                        out=p2[:], lhsT=w2_codes[:, a, t, :].bitcast(FP4X4), lhsT_scale=w2_plane[:, a, t, :],
+                        rhs=v_codes[a, h][:].bitcast(FP8X4), rhs_scale=v_plane[a][:, cols],
+                        start=(a == 0), stop=(a == PASSES - 1),
+                    )
+                for a in range(PASSES):
+                    nc.tensor.matmul_mx(
+                        out=p1[:], lhsT=w1_q[a][0][:, rows].bitcast(FP8X4), lhsT_scale=w1_q[a][1][:, rows],
+                        rhs=v_codes[a, h][:].bitcast(FP8X4), rhs_scale=v_plane[a][:, cols],
+                        start=(a == 0), stop=(a == PASSES - 1),
+                    )
+                first_sum[t, h] = p1
+                second_sum[t, h] = held("second%d%d" % (t, h), [P, HALF], F32)
+                nc.scalar.copy(out=second_sum[t, h][:], in_=p2[:])
+
+        def readings(t):
+            larger[t] = keep.tile([P, S], F32, name="larger%d" % t, tag="ring%d" % (SLOT_ORDER.index(t) % 2))
+            for h in range(S // HALF):
+                nc.vector.tensor_tensor(
+                    out=larger[t][:, h * HALF : (h + 1) * HALF], in0=first_sum[t, h][:], in1=second_sum[t, h][:],
+                    op=ALU.max,
+                )
+
+        def overwrite(t):
+            nc.vector.tensor_tensor(page[t][:].indirect(list2[:]), larger[t][:], factor[t][:], ALU.mult)
+
+        def fetch_mover(t):
+            mover[t] = work.tile([P, PAIRS], F32, name="mover")
+            nc.vector.tensor_copy(mover[t][:], page[t][:].indirect(list3[:]))
+
+        def fetch_opponent(t):
+            later = SLOT_ORDER.index(t) + 2
+            tag = "page%d" % SLOT_ORDER[later] if later < PACK else "opponent%d" % t
+            opponent[t] = keep.tile([P, PAIRS], F32, name="opponent%d" % t, tag=tag)
+            nc.vector.tensor_copy(opponent[t][:], page[t][:].indirect(list4[:]))
+            mixed[t] = work.tile([P, PAIRS], F32, name="mixed")
+            nc.gpsimd.tensor_scalar(mixed[t][:], opponent[t][:], mix_col[:, t : t + 1], 0.0, ALU.mult, ALU.add)
+
+        def compare(t):
+            top[t] = keep.tile([P, PAIRS], F32, name="top%d" % t, tag="ring%d" % ((SLOT_ORDER.index(t) + 1) % 2))
+            nc.vector.tensor_tensor(out=top[t][:], in0=mover[t][:], in1=opponent[t][:], op=ALU.max)
+
+        def put_opponent(t):
+            nc.vector.tensor_copy(page[t][:].indirect(list4[:]), top[t][:])
+
+        def put_mover(t):
+            nc.vector.tensor_tensor(page[t][:].indirect(list3[:]), mover[t][:], mixed[t][:], ALU.add)
+
+        def weave(t, c, on_vector):
+            src = page[t][:, STARTS[c] : STARTS[c] + WIDTHS[c]]
+            if on_vector:
+                nc.vector.tensor_copy(out=woven[c][:, :, t], in_=src)
+            else:
+                nc.scalar.copy(out=woven[c][:, :, t], in_=src)
+
+        first, last = SLOT_ORDER[0], SLOT_ORDER[-1]
+        rest_q, woven = [], []
+        products(first)
+        readings(first)
+        rest_q.extend(quantize_weight("w1_rest%d" % a, w1_rest[a], "w1_rest_codes%d" % a) for a in range(PASSES))
+        for t in SLOT_ORDER[1:]:
+            products(t)
+        overwrite(first)
+        readings(SLOT_ORDER[1])
+        fetch_opponent(first)
+        fetch_mover(first)
+        for i, t in enumerate(SLOT_ORDER[:-1]):
+            ahead = SLOT_ORDER[i + 1]
+            overwrite(ahead)
+            if i + 2 < PACK:
+                readings(SLOT_ORDER[i + 2])
+            else:
+                w3_codes, w3_plane = quantize_weight("w3", w3_grouped, "factor%d" % last)
+            compare(t)
+            if i + 2 < PACK:
+                load_page(SLOT_ORDER[i + 2])
+            fetch_opponent(ahead)
+            put_opponent(t)
+            fetch_mover(ahead)
+            put_mover(t)
+            if i == 0:
+                spent = ["w1_rest_codes0"] + ["v_codes%d%d" % (a, h) for a in range(PASSES) for h in range(2)]
+                spent = spent + ["second%d%d" % (u, h) for u in SLOT_ORDER[2:] for h in range(2)]
+                woven.extend(
+                    keep.tile([P, WIDTHS[c], PACK], BF16, name="woven%d" % c, tag=spent[c], align_bytes=64)
+                    for c in range(CHUNKS)
+                )
+            for c in range(CHUNKS):
+                weave(t, c, False)
+        compare(last)
+        put_opponent(last)
+        put_mover(last)
+
+        out_rows = out.rearrange("(j p) c -> p j c", p=P)
+        for c in range(VECTOR_ROUNDED_CHUNKS, CHUNKS):
+            weave(last, c, False)
+        for c in range(CHUNKS):
+            width = WIDTHS[c]
+            if c < VECTOR_ROUNDED_CHUNKS:
+                weave(last, c, True)
+            b_codes = work.tile([P, width], U32, name="b_codes", bufs=CHUNKS, align_bytes=64)
+            b_plane = work.tile([P, width], U8, name="b_plane", bufs=CHUNKS, align_bytes=64)
+            nc.vector.quantize_mx(
+                out=b_codes[:].bitcast(FP8X4), scales=b_plane[:], in_=woven[c][:].rearrange("p n t -> p (n t)")
+            )
+            y = work.tile([P, width, PACK], F32, name="y", bufs=3)
+            for s in range(width // SUB):
+                cols = slice(s * SUB, (s + 1) * SUB)
+                sums = psum.tile([P, PACK, SUB], F32, name="bank_a")
+                for t in range(PACK):
+                    rows = slice(t * SUB, (t + 1) * SUB)
+                    nc.tensor.matmul_mx(
+                        out=sums[:, t, :], lhsT=w3_codes[:, rows].bitcast(FP8X4), lhsT_scale=w3_plane[:, rows],
+                        rhs=b_codes[:, cols].bitcast(FP8X4), rhs_scale=b_plane[:, cols], start=True, stop=True,
+                    )
+                nc.scalar.activation(out=y[:, cols, :], in_=sums[:].rearrange("p t n -> p n t"), func=ACT.Tanh)
+            z = work.tile([P, width, PACK], BF16, name="z", bufs=3, align_bytes=64)
+            nc.vector.tensor_tensor(
+                out=z[:], in0=y[:], in1=lift_col[:].unsqueeze(1).to_broadcast([P, width, PACK]), op=ALU.mult
+            )
+            z_codes = work.tile([P, width], U32, name="z_codes", bufs=3, align_bytes=64)
+            z_plane = work.tile([P, width], U8, name="z_plane", bufs=3, align_bytes=64)
+            nc.vector.quantize_mx(
+                out=z_codes[:].bitcast(FP8X4), scales=z_plane[:], in_=z[:].rearrange("p n t -> p (n t)")
+            )
+            scores = psum.tile([P, N // P, width], F32, name="bank_b")
+            for j in range(N // P):
+                nc.tensor.matmul_mx(
+                    out=scores[:, j, :], lhsT=w4_codes[:, 2 * P * j : 2 * P * (j + 1)].bitcast(FP4X4),
+                    lhsT_scale=w4_plane[:, 0, P * j : P * (j + 1)],
+                    rhs=z_codes[:].bitcast(FP8X4), rhs_scale=z_plane[:], start=True, stop=True,
+                )
+            staged = work.tile([P, N // P, width], F32, name="staged", bufs=4)
+            nc.scalar.copy(out=staged[:], in_=scores[:])
+            nc.sync.dma_start(out=out_rows[:, :, STARTS[c] : STARTS[c] + width], in_=staged[:])

@@ -37,7 +37,7 @@ def tile_list_cube_cache_scores_kernel(
     with ExitStack() as ctx:
         keep = ctx.enter_context(tc.tile_pool(name="keep", bufs=1))
         work = ctx.enter_context(tc.tile_pool(name="work", bufs=2))
-        psum = ctx.enter_context(tc.psum_pool(name="psum", bufs=4))
+        psum = ctx.enter_context(tc.psum_pool(name="psum", bufs=1))
 
         def held(name, shape, dtype):
             return keep.tile(shape, dtype, name=name, align_bytes=64)
@@ -100,7 +100,7 @@ def tile_list_cube_cache_scores_kernel(
         )
         w2_raw = held("w2_raw", [P, PASSES, 2 * H], U8)
         nc.sync.dma_start(out=w2_raw[:].bitcast(I32), in_=w2_words.rearrange("a p c -> p a c").bitcast(I32))
-        load_scale_rows(nc.scalar, w2_plane_raw, w2_scales)
+        load_scale_rows(nc.gpsimd, w2_plane_raw, w2_scales)
         tab = [held("tab%d" % a, [P, T], I32) for a in range(PASSES)]
         for a in range(PASSES):
             nc.sync.dma_start(out=tab[a][:], in_=tab_words[a].rearrange("p t i -> p (t i)").bitcast(I32))
@@ -182,8 +182,9 @@ def tile_list_cube_cache_scores_kernel(
             rows = slice(place * SUB, (place + 1) * SUB)
             for h in range(S // HALF):
                 cols = slice(h * HALF, (h + 1) * HALF)
-                p2 = psum.tile([P, HALF], F32, name="bank_b")
-                p1 = psum.tile([P, HALF], F32, name="bank_a")
+                turn = SLOT_ORDER.index(t)
+                p2 = psum.tile([P, HALF], F32, name="p2", tag="bank%d" % ((0, 2, 6, 6)[turn] + h))
+                p1 = psum.tile([P, HALF], F32, name="p1", tag="bank%d" % ((2, 4, 0, 2)[turn] + h))
                 for a in range(PASSES):
                     nc.tensor.matmul_mx(
                         out=p2[:], lhsT=w2_codes[:, a, t, :].bitcast(FP4X4), lhsT_scale=w2_plane[:, a, t, :],
@@ -293,7 +294,7 @@ def tile_list_cube_cache_scores_kernel(
             y = work.tile([P, width, PACK], F32, name="y", bufs=3)
             for s in range(width // SUB):
                 cols = slice(s * SUB, (s + 1) * SUB)
-                sums = psum.tile([P, PACK, SUB], F32, name="bank_a")
+                sums = psum.tile([P, PACK, SUB], F32, name="sums", tag="bank%d" % ((STARTS[c] // SUB + s) % 5))
                 for t in range(PACK):
                     rows = slice(t * SUB, (t + 1) * SUB)
                     nc.tensor.matmul_mx(
@@ -310,7 +311,7 @@ def tile_list_cube_cache_scores_kernel(
             nc.vector.quantize_mx(
                 out=z_codes[:].bitcast(FP8X4), scales=z_plane[:], in_=z[:].rearrange("p n t -> p (n t)")
             )
-            scores = psum.tile([P, N // P, width], F32, name="bank_b")
+            scores = psum.tile([P, N // P, width], F32, name="scores", tag="bank%d" % (5 + c % 3))
             for j in range(N // P):
                 nc.tensor.matmul_mx(
                     out=scores[:, j, :], lhsT=w4_codes[:, 2 * P * j : 2 * P * (j + 1)].bitcast(FP4X4),

@@ -116,7 +116,10 @@ def tile_list_cube_cache_scores_kernel(
             factor[t] = held("factor%d" % t, [P, S], F32)
             for quad in (0, 2, 1, 3):
                 nc.sync.dma_start(out=factor[t][32 * quad : 32 * quad + 32, :], in_=wgs_rows[t])
-            nc.scalar.activation(out=factor[t][:], in_=factor[t][:], func=ACT.Copy, scale=gain_col[:, t : t + 1])
+            if t == SLOT_ORDER[0]:
+                nc.vector.tensor_scalar(factor[t][:], factor[t][:], gain_col[:, t : t + 1], None, ALU.mult)
+            else:
+                nc.scalar.activation(out=factor[t][:], in_=factor[t][:], func=ACT.Copy, scale=gain_col[:, t : t + 1])
 
         def load_page(t):
             page[t] = keep.tile([P, T2], F32, name="page%d" % t, tag="page%d" % t)
@@ -154,11 +157,9 @@ def tile_list_cube_cache_scores_kernel(
 
         w2_codes = held("w2_codes", [P, PASSES, PACK, 2 * SUB], U8)
         w2_plane = held("w2_plane", [P, PASSES, PACK, SUB], U8)
-        for a in range(PASSES):
-            nc.vector.tensor_copy(
-                out=w2_codes[:, a].rearrange("p t (m b) -> p t m b", b=2),
-                in_=w2_raw[:, a].rearrange("p (m t b) -> p t m b", t=PACK, b=2),
-            )
+        nc.vector.tensor_copy(
+            out=w2_codes[:].bitcast(U16), in_=w2_raw[:].bitcast(U16).rearrange("p a (m t) -> p a t m", t=PACK)
+        )
         gather_words(0)
         nc.vector.tensor_copy(out=w2_plane[:], in_=w2_plane_raw[:].rearrange("p a (m t) -> p a t m", t=PACK))
         gather_words(1)
@@ -176,6 +177,7 @@ def tile_list_cube_cache_scores_kernel(
 
         larger, mover, opponent, mixed, top = {}, {}, {}, {}, {}
         first_sum, second_sum = {}, {}
+        ring = ("larger", "factor%d" % SLOT_ORDER[0])
 
         def products(t):
             w1_q, place = (lead_q, 0) if t == 0 else (rest_q, t - 1)
@@ -202,7 +204,7 @@ def tile_list_cube_cache_scores_kernel(
                 nc.scalar.copy(out=second_sum[t, h][:], in_=p2[:])
 
         def readings(t):
-            larger[t] = keep.tile([P, S], F32, name="larger%d" % t, tag="ring%d" % (SLOT_ORDER.index(t) % 2))
+            larger[t] = keep.tile([P, S], F32, name="larger%d" % t, tag=ring[SLOT_ORDER.index(t) % 2], align_bytes=64)
             for h in range(S // HALF):
                 nc.vector.tensor_tensor(
                     out=larger[t][:, h * HALF : (h + 1) * HALF], in0=first_sum[t, h][:], in1=second_sum[t, h][:],
@@ -222,10 +224,11 @@ def tile_list_cube_cache_scores_kernel(
             opponent[t] = keep.tile([P, PAIRS], F32, name="opponent%d" % t, tag=tag)
             nc.vector.tensor_copy(opponent[t][:], page[t][:].indirect(list4[:]))
             mixed[t] = work.tile([P, PAIRS], F32, name="mixed")
-            nc.gpsimd.tensor_scalar(mixed[t][:], opponent[t][:], mix_col[:, t : t + 1], 0.0, ALU.mult, ALU.add)
+            if t != SLOT_ORDER[0]:
+                nc.scalar.activation(out=mixed[t][:], in_=opponent[t][:], func=ACT.Copy, scale=mix_col[:, t : t + 1])
 
         def compare(t):
-            top[t] = keep.tile([P, PAIRS], F32, name="top%d" % t, tag="ring%d" % ((SLOT_ORDER.index(t) + 1) % 2))
+            top[t] = keep.tile([P, PAIRS], F32, name="top%d" % t, tag=ring[(SLOT_ORDER.index(t) + 1) % 2], align_bytes=64)
             nc.vector.tensor_tensor(out=top[t][:], in0=mover[t][:], in1=opponent[t][:], op=ALU.max)
 
         def put_opponent(t):
@@ -252,6 +255,7 @@ def tile_list_cube_cache_scores_kernel(
         readings(SLOT_ORDER[1])
         fetch_opponent(first)
         fetch_mover(first)
+        nc.vector.tensor_scalar(mixed[first][:], opponent[first][:], mix_col[:, first : first + 1], None, ALU.mult)
         for i, t in enumerate(SLOT_ORDER[:-1]):
             ahead = SLOT_ORDER[i + 1]
             overwrite(ahead)

@@ -36,11 +36,15 @@ def tile_list_cube_cache_scores_kernel(
     nc = tc.nc
     with ExitStack() as ctx:
         keep = ctx.enter_context(tc.tile_pool(name="keep", bufs=1))
+        relay = ctx.enter_context(tc.tile_pool(name="relay", bufs=1))
         work = ctx.enter_context(tc.tile_pool(name="work", bufs=2))
         psum = ctx.enter_context(tc.psum_pool(name="psum", bufs=1))
 
         def held(name, shape, dtype):
             return keep.tile(shape, dtype, name=name, align_bytes=64)
+
+        def placed(name, shape, dtype, kib):
+            return relay.tile(shape, dtype, name=name, align_bytes=64, offset=int(kib * 1024))
 
         def load_scale_rows(queue, plane, scales):
             for quad in range(4):
@@ -54,19 +58,19 @@ def tile_list_cube_cache_scores_kernel(
             nc.sync.dma_start(lst[:], src)
             return lst
 
-        def load_per_row(queue, name, vec):
-            col = held(name, [P, PACK], F32)
-            queue.dma_start(out=col[:], in_=vec.rearrange("(p t) -> p t", t=PACK))
+        def load_per_row(name, vec, kib):
+            col = placed(name, [P, PACK], F32, kib)
+            nc.sync.dma_start(out=col[:], in_=vec.rearrange("(p t) -> p t", t=PACK))
             return col
 
-        def load_weight(rows):
-            raw = work.tile([P, PACK, H], F32, name="raw", align_bytes=64)
+        def load_weight(name, rows, kib):
+            raw = placed(name, [P, PACK, H], F32, kib)
             nc.sync.dma_start(out=raw[:], in_=rows.rearrange("(p j) c -> p j c", j=PACK))
             return raw
 
-        def group_weight(name, raw, slots, on_vector):
+        def group_weight(name, raw, slots, on_vector, kib):
             count = slots.stop - slots.start
-            grouped = held(name + "_grouped", [P, count, SUB, PACK], BF16)
+            grouped = placed(name + "_grouped", [P, count, SUB, PACK], BF16, kib)
             dst = grouped[:].rearrange("p t m j -> p m t j")
             src = raw[:].rearrange("p j (m t) -> p m t j", t=PACK)[:, :, slots, :]
             if on_vector:
@@ -75,9 +79,8 @@ def tile_list_cube_cache_scores_kernel(
                 nc.scalar.copy(out=dst, in_=src)
             return grouped
 
-        def quantize_weight(name, grouped, codes_tag):
+        def quantize_weight(name, grouped, codes):
             width = grouped.shape[1] * SUB
-            codes = keep.tile([P, width], U32, name=name + "_codes", tag=codes_tag, align_bytes=64)
             plane = held(name + "_plane", [P, width], U8)
             nc.vector.quantize_mx(
                 out=codes[:].bitcast(FP8X4), scales=plane[:], in_=grouped[:].rearrange("p t m j -> p (t m j)")
@@ -91,58 +94,27 @@ def tile_list_cube_cache_scores_kernel(
         v_plane = [held("v_plane%d" % a, [P, S], U8) for a in range(PASSES)]
         for a in range(PASSES):
             nc.gpsimd.memset(v_plane[a][:].bitcast(I32), 0)
-        w4_plane = held("w4_plane", [P, 1, N], U8)
-        nc.gpsimd.memset(w4_plane[:].bitcast(I32), 0)
 
         list1 = load_list("list1", offs, S)
         nc.sync.dma_start(
             out=tab_rows[96:P, :].bitcast(I32), in_=tab_scales.rearrange("a q t -> (a q) t").bitcast(I32)
         )
-        w2_raw = held("w2_raw", [P, PASSES, 2 * H], U8)
+        w2_raw = placed("w2_raw", [P, PASSES, 2 * H], U8, 32)
         nc.sync.dma_start(out=w2_raw[:].bitcast(I32), in_=w2_words.rearrange("a p c -> p a c").bitcast(I32))
         load_scale_rows(nc.gpsimd, w2_plane_raw, w2_scales)
-        tab = [held("tab%d" % a, [P, T], I32) for a in range(PASSES)]
-        for a in range(PASSES):
-            nc.sync.dma_start(out=tab[a][:], in_=tab_words[a].rearrange("p t i -> p (t i)").bitcast(I32))
-        w1_raw = [load_weight(w1[a * P * PACK : (a + 1) * P * PACK, :]) for a in range(PASSES)]
-        lead, rest = slice(0, 1), slice(1, PACK)
-        w1_lead = [group_weight("w1_lead0", w1_raw[0], lead, False)]
-
-        wgs_rows = wgs.rearrange("(q t) j -> t q j", t=PACK)
-        page_rows = page0.rearrange("(p t) c -> t p c", t=PACK)
-        factor, page = {}, {}
-
-        def load_factor(t):
-            factor[t] = held("factor%d" % t, [P, S], F32)
-            for quad in (0, 2, 1, 3):
-                nc.sync.dma_start(out=factor[t][32 * quad : 32 * quad + 32, :], in_=wgs_rows[t])
-            if t == SLOT_ORDER[0]:
-                nc.vector.tensor_scalar(factor[t][:], factor[t][:], gain_col[:, t : t + 1], None, ALU.mult)
-            else:
-                nc.scalar.activation(out=factor[t][:], in_=factor[t][:], func=ACT.Copy, scale=gain_col[:, t : t + 1])
-
-        def load_page(t):
-            page[t] = keep.tile([P, T2], F32, name="page%d" % t, tag="page%d" % t)
-            nc.sync.dma_start(out=page[t][:], in_=page_rows[t])
-
-        gain_col = load_per_row(nc.sync, "gain_col", gain)
-        load_factor(SLOT_ORDER[0])
-        load_page(SLOT_ORDER[0])
         list2 = load_list("list2", offs2, S)
         list3 = load_list("list3", offs3, PAIRS)
         list4 = load_list("list4", offs4, PAIRS)
-        mix_col = load_per_row(nc.sync, "mix_col", mix)
-        w1_rest = [group_weight("w1_rest0", w1_raw[0], rest, False)]
-        load_factor(SLOT_ORDER[1])
-        load_factor(SLOT_ORDER[2])
-        load_page(SLOT_ORDER[1])
+        tab = [placed("tab%d" % a, [P, T], I32, 16 * a) for a in range(PASSES)]
+        for a in range(PASSES):
+            nc.sync.dma_start(out=tab[a][:], in_=tab_words[a].rearrange("p t i -> p (t i)").bitcast(I32))
 
         picked_rows = held("picked_rows", [P, S], U8)
         nc.vector.tensor_copy(picked_rows[:], tab_rows[:].indirect(list1[:]))
         for a in range(PASSES):
             for quad in range(4):
                 row = 96 + 16 * a + 4 * quad
-                nc.gpsimd.dma_start(
+                nc.scalar.dma_start(
                     out=v_plane[a][32 * quad : 32 * quad + 4, :].bitcast(I32),
                     in_=picked_rows[row : row + 4, :].bitcast(I32),
                 )
@@ -163,21 +135,43 @@ def tile_list_cube_cache_scores_kernel(
         gather_words(0)
         nc.vector.tensor_copy(out=w2_plane[:], in_=w2_plane_raw[:].rearrange("p a (m t) -> p a t m", t=PACK))
         gather_words(1)
-        w1_lead.append(group_weight("w1_lead1", w1_raw[1], lead, True))
-        lead_q = [quantize_weight("w1_lead%d" % a, w1_lead[a], "w1_lead_codes%d" % a) for a in range(PASSES)]
-        w1_rest.append(group_weight("w1_rest1", w1_raw[1], rest, True))
 
-        w3_raw = load_weight(w3)
-        w3_grouped = group_weight("w3", w3_raw, slice(0, PACK), False)
-        load_factor(SLOT_ORDER[3])
-        lift_col = load_per_row(nc.sync, "lift_col", lift)
-        w4_codes = held("w4_codes", [P, 2 * N], U8)
-        nc.sync.dma_start(out=w4_codes[:].bitcast(I32), in_=w4_words[0].bitcast(I32))
-        load_scale_rows(nc.sync, w4_plane, w4_scales)
+        w1_raw = [load_weight("w1_raw%d" % a, w1[a * P * PACK : (a + 1) * P * PACK, :], (32, 0)[a]) for a in range(PASSES)]
+        lead, rest = slice(0, 1), slice(1, PACK)
+        w1_lead = [group_weight("w1_lead0", w1_raw[0], lead, False, 43)]
+
+        wgs_rows = wgs.rearrange("(q t) j -> t q j", t=PACK)
+        page_rows = page0.rearrange("(p t) c -> t p c", t=PACK)
+        factor, page = {}, {}
+
+        def load_factor(t):
+            factor[t] = placed("factor%d" % t, [P, S], F32, (8, 24, 28, 40)[SLOT_ORDER.index(t)])
+            for quad in (0, 2, 1, 3):
+                nc.sync.dma_start(out=factor[t][32 * quad : 32 * quad + 32, :], in_=wgs_rows[t])
+            if t == SLOT_ORDER[0]:
+                nc.vector.tensor_scalar(factor[t][:], factor[t][:], gain_col[:, t : t + 1], None, ALU.mult)
+            else:
+                nc.scalar.activation(out=factor[t][:], in_=factor[t][:], func=ACT.Copy, scale=gain_col[:, t : t + 1])
+
+        def load_page(t):
+            turn = SLOT_ORDER.index(t)
+            if turn < 2:
+                page[t] = placed("page%d" % t, [P, T2], F32, (16, 32)[turn])
+            else:
+                page[t] = keep.tile([P, T2], F32, name="page%d" % t, tag="page%d" % t)
+            nc.sync.dma_start(out=page[t][:], in_=page_rows[t])
+
+        gain_col = load_per_row("gain_col", gain, 12)
+        load_factor(SLOT_ORDER[0])
+        load_page(SLOT_ORDER[0])
+        mix_col = load_per_row("mix_col", mix, 12.5)
+
+        w1_lead.append(group_weight("w1_lead1", w1_raw[1], lead, True, 47))
+        lead_q = [quantize_weight("w1_lead%d" % a, w1_lead[a], held("w1_lead_codes%d" % a, [P, SUB], U32)) for a in range(PASSES)]
 
         larger, mover, opponent, mixed, top = {}, {}, {}, {}, {}
         first_sum, second_sum = {}, {}
-        ring = ("larger", "factor%d" % SLOT_ORDER[0])
+        ring = (52, 8)
 
         def products(t):
             w1_q, place = (lead_q, 0) if t == 0 else (rest_q, t - 1)
@@ -204,7 +198,7 @@ def tile_list_cube_cache_scores_kernel(
                 nc.scalar.copy(out=second_sum[t, h][:], in_=p2[:])
 
         def readings(t):
-            larger[t] = keep.tile([P, S], F32, name="larger%d" % t, tag=ring[SLOT_ORDER.index(t) % 2], align_bytes=64)
+            larger[t] = placed("larger%d" % t, [P, S], F32, ring[SLOT_ORDER.index(t) % 2])
             for h in range(S // HALF):
                 nc.vector.tensor_tensor(
                     out=larger[t][:, h * HALF : (h + 1) * HALF], in0=first_sum[t, h][:], in1=second_sum[t, h][:],
@@ -228,7 +222,7 @@ def tile_list_cube_cache_scores_kernel(
                 nc.scalar.activation(out=mixed[t][:], in_=opponent[t][:], func=ACT.Copy, scale=mix_col[:, t : t + 1])
 
         def compare(t):
-            top[t] = keep.tile([P, PAIRS], F32, name="top%d" % t, tag=ring[(SLOT_ORDER.index(t) + 1) % 2], align_bytes=64)
+            top[t] = placed("top%d" % t, [P, PAIRS], F32, ring[(SLOT_ORDER.index(t) + 1) % 2])
             nc.vector.tensor_tensor(out=top[t][:], in0=mover[t][:], in1=opponent[t][:], op=ALU.max)
 
         def put_opponent(t):
@@ -248,21 +242,35 @@ def tile_list_cube_cache_scores_kernel(
         rest_q, woven = [], []
         products(first)
         readings(first)
-        rest_q.extend(quantize_weight("w1_rest%d" % a, w1_rest[a], "w1_rest_codes%d" % a) for a in range(PASSES))
+        w1_rest = [group_weight("w1_rest%d" % a, w1_raw[a], rest, False, (40, 44)[a]) for a in range(PASSES)]
+        load_factor(SLOT_ORDER[1])
+        load_factor(SLOT_ORDER[2])
+        load_page(SLOT_ORDER[1])
+        overwrite(first)
+        rest_q.extend(quantize_weight("w1_rest%d" % a, w1_rest[a], placed("w1_rest_codes%d" % a, [P, H - SUB], U32, 52 + 1.5 * a)) for a in range(PASSES))
+        w3_raw = load_weight("w3_raw", w3, 0)
+        w3_grouped = group_weight("w3", w3_raw, slice(0, PACK), False, 48)
+        load_factor(SLOT_ORDER[3])
+        lift_col = load_per_row("lift_col", lift, 44)
+        w4_codes = placed("w4_codes", [P, 2 * N], U8, 44.5)
+        nc.sync.dma_start(out=w4_codes[:].bitcast(I32), in_=w4_words[0].bitcast(I32))
+        w4_plane = placed("w4_plane", [P, 1, N], U8, 45)
+        nc.gpsimd.memset(w4_plane[:].bitcast(I32), 0)
+        load_scale_rows(nc.sync, w4_plane, w4_scales)
+
         for t in SLOT_ORDER[1:]:
             products(t)
-        overwrite(first)
-        readings(SLOT_ORDER[1])
         fetch_opponent(first)
         fetch_mover(first)
         nc.vector.tensor_scalar(mixed[first][:], opponent[first][:], mix_col[:, first : first + 1], None, ALU.mult)
+        readings(SLOT_ORDER[1])
         for i, t in enumerate(SLOT_ORDER[:-1]):
             ahead = SLOT_ORDER[i + 1]
             overwrite(ahead)
             if i + 2 < PACK:
                 readings(SLOT_ORDER[i + 2])
             else:
-                w3_codes, w3_plane = quantize_weight("w3", w3_grouped, "factor%d" % last)
+                w3_codes, w3_plane = quantize_weight("w3", w3_grouped, placed("w3_codes", [P, M], U32, 40))
             compare(t)
             if i + 2 < PACK:
                 load_page(SLOT_ORDER[i + 2])
@@ -271,7 +279,7 @@ def tile_list_cube_cache_scores_kernel(
             fetch_mover(ahead)
             put_mover(t)
             if i == 0:
-                spent = ["w1_rest_codes0"] + ["v_codes%d%d" % (a, h) for a in range(PASSES) for h in range(2)]
+                spent = ["w1_rest0_plane"] + ["v_codes%d%d" % (a, h) for a in range(PASSES) for h in range(2)]
                 spent = spent + ["second%d%d" % (u, h) for u in SLOT_ORDER[2:] for h in range(2)]
                 woven.extend(
                     keep.tile([P, WIDTHS[c], PACK], BF16, name="woven%d" % c, tag=spent[c], align_bytes=64)

@@ -114,7 +114,7 @@ def tile_list_cube_cache_scores_kernel(
         for a in range(PASSES):
             for quad in range(4):
                 row = 96 + 16 * a + 4 * quad
-                nc.scalar.dma_start(
+                (nc.scalar, nc.gpsimd)[a].dma_start(
                     out=v_plane[a][32 * quad : 32 * quad + 4, :].bitcast(I32),
                     in_=picked_rows[row : row + 4, :].bitcast(I32),
                 )
@@ -288,8 +288,8 @@ def tile_list_cube_cache_scores_kernel(
             for c in range(CHUNKS):
                 weave(t, c, False)
         compare(last)
-        put_opponent(last)
         put_mover(last)
+        put_opponent(last)
 
         out_rows = out.rearrange("(j p) c -> p j c", p=P)
         for c in range(VECTOR_ROUNDED_CHUNKS, CHUNKS):

from contextlib import ExitStack

import concourse.mybir as mybir

K, H, M, N, T, S, T2, PAIRS = 1024, 512, 512, 256, 4096, 1024, 2048, 512
FLOPS = 2 * (2 * K * H * S + H * M * T2 + M * N * T2)

F32 = mybir.dt.float32
BF16 = mybir.dt.bfloat16
I32 = mybir.dt.int32
U32 = mybir.dt.uint32
U16 = mybir.dt.uint16
U8 = mybir.dt.uint8
FP8X4 = mybir.dt.float8_e4m3fn_x4
FP4X4 = mybir.dt.float4_e2m1fn_x4
ALU = mybir.AluOpType
ACT = mybir.ActivationFunctionType

P = 128
PACK = 4
PASSES = K // (P * PACK)
HALF = 512
CHUNK = 256
WIDTHS = (CHUNK // 2,) + (CHUNK,) * (T2 // CHUNK - 1) + (CHUNK // 2,)
STARTS = tuple(sum(WIDTHS[:c]) for c in range(len(WIDTHS)))
CHUNKS = len(WIDTHS)
SUB = 128
SLOT_ORDER = (0, 2, 3, 1)
VECTOR_ROUNDED_CHUNKS = 6


def tile_list_cube_cache_scores_kernel(
    tc, tab_words, tab_scales, offs, offs2, offs3, offs4, w1, w2_words, w2_scales,
    gain, wgs, page0, mix, w3, lift, w4_words, w4_scales, out,
):
    nc = tc.nc
    with ExitStack() as ctx:
        keep = ctx.enter_context(tc.tile_pool(name="keep", bufs=1))
        relay = ctx.enter_context(tc.tile_pool(name="relay", bufs=1))
        work = ctx.enter_context(tc.tile_pool(name="work", bufs=2))
        psum = ctx.enter_context(tc.psum_pool(name="psum", bufs=1))

        def held(name, shape, dtype):
            return keep.tile(shape, dtype, name=name, align_bytes=64)

        def placed(name, shape, dtype, kib):
            return relay.tile(shape, dtype, name=name, align_bytes=64, offset=int(kib * 1024))

        def load_scale_rows(queue, plane, scales):
            for quad in range(4):
                queue.dma_start(
                    out=plane[32 * quad : 32 * quad + 4, :, :].bitcast(I32),
                    in_=scales[:, 4 * quad : 4 * quad + 4, :].rearrange("a r c -> r a c").bitcast(I32),
                )

        def load_list(name, src, entries):
            lst = keep.tile([P, entries // 16], U16, name=name)
            nc.sync.dma_start(lst[:], src)
            return lst

        def load_per_row(name, vec, kib):
            col = placed(name, [P, PACK], F32, kib)
            nc.sync.dma_start(out=col[:], in_=vec.rearrange("(p t) -> p t", t=PACK))
            return col

        def load_weight(name, rows, kib):
            raw = placed(name, [P, PACK, H], F32, kib)
            nc.sync.dma_start(out=raw[:], in_=rows.rearrange("(p j) c -> p j c", j=PACK))
            return raw

        def group_weight(name, raw, slots, on_vector, kib):
            count = slots.stop - slots.start
            grouped = placed(name + "_grouped", [P, count, SUB, PACK], BF16, kib)
            dst = grouped[:].rearrange("p t m j -> p m t j")
            src = raw[:].rearrange("p j (m t) -> p m t j", t=PACK)[:, :, slots, :]
            if on_vector:
                nc.vector.tensor_copy(out=dst, in_=src)
            else:
                nc.scalar.copy(out=dst, in_=src)
            return grouped

        def quantize_weight(name, grouped, codes):
            width = grouped.shape[1] * SUB
            plane = held(name + "_plane", [P, width], U8)
            nc.vector.quantize_mx(
                out=codes[:].bitcast(FP8X4), scales=plane[:], in_=grouped[:].rearrange("p t m j -> p (t m j)")
            )
            return codes, plane

        tab_rows = held("tab_rows", [P, T], U8)
        nc.vector.memset(tab_rows[0:96, :].bitcast(I32), 0)
        w2_plane_raw = held("w2_plane_raw", [P, PASSES, H], U8)
        nc.gpsimd.memset(w2_plane_raw[:].bitcast(I32), 0)
        v_plane = [held("v_plane%d" % a, [P, S], U8) for a in range(PASSES)]
        for a in range(PASSES):
            nc.gpsimd.memset(v_plane[a][:].bitcast(I32), 0)

        list1 = load_list("list1", offs, S)
        nc.sync.dma_start(
            out=tab_rows[96:P, :].bitcast(I32), in_=tab_scales.rearrange("a q t -> (a q) t").bitcast(I32)
        )
        w2_raw = placed("w2_raw", [P, PASSES, 2 * H], U8, 32)
        nc.sync.dma_start(out=w2_raw[:].bitcast(I32), in_=w2_words.rearrange("a p c -> p a c").bitcast(I32))
        load_scale_rows(nc.gpsimd, w2_plane_raw, w2_scales)
        list2 = load_list("list2", offs2, S)
        list3 = load_list("list3", offs3, PAIRS)
        list4 = load_list("list4", offs4, PAIRS)
        tab = [placed("tab%d" % a, [P, T], I32, 16 * a) for a in range(PASSES)]
        for a in range(PASSES):
            nc.sync.dma_start(out=tab[a][:], in_=tab_words[a].rearrange("p t i -> p (t i)").bitcast(I32))

        picked_rows = held("picked_rows", [P, S], U8)
        nc.vector.tensor_copy(picked_rows[:], tab_rows[:].indirect(list1[:]))
        for a in range(PASSES):
            for quad in range(4):
                row = 96 + 16 * a + 4 * quad
                (nc.scalar, nc.gpsimd)[a].dma_start(
                    out=v_plane[a][32 * quad : 32 * quad + 4, :].bitcast(I32),
                    in_=picked_rows[row : row + 4, :].bitcast(I32),
                )

        v_codes = {}

        def gather_words(a):
            for h in range(S // HALF):
                v_codes[a, h] = held("v_codes%d%d" % (a, h), [P, HALF], U32)
                cols = slice(h * HALF // 16, (h + 1) * HALF // 16)
                nc.vector.tensor_copy(v_codes[a, h][:], tab[a][:].bitcast(U32).indirect(list1[:, cols]))

        w2_codes = held("w2_codes", [P, PASSES, PACK, 2 * SUB], U8)
        w2_plane = held("w2_plane", [P, PASSES, PACK, SUB], U8)
        nc.vector.tensor_copy(
            out=w2_codes[:].bitcast(U16), in_=w2_raw[:].bitcast(U16).rearrange("p a (m t) -> p a t m", t=PACK)
        )
        gather_words(0)
        nc.vector.tensor_copy(out=w2_plane[:], in_=w2_plane_raw[:].rearrange("p a (m t) -> p a t m", t=PACK))
        gather_words(1)

        w1_raw = [load_weight("w1_raw%d" % a, w1[a * P * PACK : (a + 1) * P * PACK, :], (32, 0)[a]) for a in range(PASSES)]
        lead, rest = slice(0, 1), slice(1, PACK)
        w1_lead = [group_weight("w1_lead0", w1_raw[0], lead, False, 43)]

        wgs_rows = wgs.rearrange("(q t) j -> t q j", t=PACK)
        page_rows = page0.rearrange("(p t) c -> t p c", t=PACK)
        factor, page = {}, {}

        def load_factor(t):
            factor[t] = placed("factor%d" % t, [P, S], F32, (8, 24, 28, 40)[SLOT_ORDER.index(t)])
            for quad in (0, 2, 1, 3):
                nc.sync.dma_start(out=factor[t][32 * quad : 32 * quad + 32, :], in_=wgs_rows[t])
            if t == SLOT_ORDER[0]:
                nc.vector.tensor_scalar(factor[t][:], factor[t][:], gain_col[:, t : t + 1], None, ALU.mult)
            else:
                nc.scalar.activation(out=factor[t][:], in_=factor[t][:], func=ACT.Copy, scale=gain_col[:, t : t + 1])

        def load_page(t):
            turn = SLOT_ORDER.index(t)
            if turn < 2:
                page[t] = placed("page%d" % t, [P, T2], F32, (16, 32)[turn])
            else:
                page[t] = keep.tile([P, T2], F32, name="page%d" % t, tag="page%d" % t)
            nc.sync.dma_start(out=page[t][:], in_=page_rows[t])

        gain_col = load_per_row("gain_col", gain, 12)
        load_factor(SLOT_ORDER[0])
        load_page(SLOT_ORDER[0])
        mix_col = load_per_row("mix_col", mix, 12.5)

        w1_lead.append(group_weight("w1_lead1", w1_raw[1], lead, True, 47))
        lead_q = [quantize_weight("w1_lead%d" % a, w1_lead[a], held("w1_lead_codes%d" % a, [P, SUB], U32)) for a in range(PASSES)]

        larger, mover, opponent, mixed, top = {}, {}, {}, {}, {}
        first_sum, second_sum = {}, {}
        ring = (52, 8)

        def products(t):
            w1_q, place = (lead_q, 0) if t == 0 else (rest_q, t - 1)
            rows = slice(place * SUB, (place + 1) * SUB)
            for h in range(S // HALF):
                cols = slice(h * HALF, (h + 1) * HALF)
                turn = SLOT_ORDER.index(t)
                p2 = psum.tile([P, HALF], F32, name="p2", tag="bank%d" % ((0, 2, 6, 6)[turn] + h))
                p1 = psum.tile([P, HALF], F32, name="p1", tag="bank%d" % ((2, 4, 0, 2)[turn] + h))
                for a in range(PASSES):
                    nc.tensor.matmul_mx(
                        out=p2[:], lhsT=w2_codes[:, a, t, :].bitcast(FP4X4), lhsT_scale=w2_plane[:, a, t, :],
                        rhs=v_codes[a, h][:].bitcast(FP8X4), rhs_scale=v_plane[a][:, cols],
                        start=(a == 0), stop=(a == PASSES - 1),
                    )
                for a in range(PASSES):
                    nc.tensor.matmul_mx(
                        out=p1[:], lhsT=w1_q[a][0][:, rows].bitcast(FP8X4), lhsT_scale=w1_q[a][1][:, rows],
                        rhs=v_codes[a, h][:].bitcast(FP8X4), rhs_scale=v_plane[a][:, cols],
                        start=(a == 0), stop=(a == PASSES - 1),
                    )
                first_sum[t, h] = p1
                second_sum[t, h] = held("second%d%d" % (t, h), [P, HALF], F32)
                nc.scalar.copy(out=second_sum[t, h][:], in_=p2[:])

        def readings(t):
            larger[t] = placed("larger%d" % t, [P, S], F32, ring[SLOT_ORDER.index(t) % 2])
            for h in range(S // HALF):
                nc.vector.tensor_tensor(
                    out=larger[t][:, h * HALF : (h + 1) * HALF], in0=first_sum[t, h][:], in1=second_sum[t, h][:],
                    op=ALU.max,
                )

        def overwrite(t):
            nc.vector.tensor_tensor(page[t][:].indirect(list2[:]), larger[t][:], factor[t][:], ALU.mult)

        def fetch_mover(t):
            mover[t] = work.tile([P, PAIRS], F32, name="mover")
            nc.vector.tensor_copy(mover[t][:], page[t][:].indirect(list3[:]))

        def fetch_opponent(t):
            later = SLOT_ORDER.index(t) + 2
            tag = "page%d" % SLOT_ORDER[later] if later < PACK else "opponent%d" % t
            opponent[t] = keep.tile([P, PAIRS], F32, name="opponent%d" % t, tag=tag)
            nc.vector.tensor_copy(opponent[t][:], page[t][:].indirect(list4[:]))
            mixed[t] = work.tile([P, PAIRS], F32, name="mixed")
            if t != SLOT_ORDER[0]:
                nc.scalar.activation(out=mixed[t][:], in_=opponent[t][:], func=ACT.Copy, scale=mix_col[:, t : t + 1])

        def compare(t):
            top[t] = placed("top%d" % t, [P, PAIRS], F32, ring[(SLOT_ORDER.index(t) + 1) % 2])
            nc.vector.tensor_tensor(out=top[t][:], in0=mover[t][:], in1=opponent[t][:], op=ALU.max)

        def put_opponent(t):
            nc.vector.tensor_copy(page[t][:].indirect(list4[:]), top[t][:])

        def put_mover(t):
            nc.vector.tensor_tensor(page[t][:].indirect(list3[:]), mover[t][:], mixed[t][:], ALU.add)

        def weave(t, c, on_vector):
            src = page[t][:, STARTS[c] : STARTS[c] + WIDTHS[c]]
            if on_vector:
                nc.vector.tensor_copy(out=woven[c][:, :, t], in_=src)
            else:
                nc.scalar.copy(out=woven[c][:, :, t], in_=src)

        first, last = SLOT_ORDER[0], SLOT_ORDER[-1]
        rest_q, woven = [], []
        products(first)
        readings(first)
        w1_rest = [group_weight("w1_rest%d" % a, w1_raw[a], rest, False, (40, 44)[a]) for a in range(PASSES)]
        load_factor(SLOT_ORDER[1])
        load_factor(SLOT_ORDER[2])
        load_page(SLOT_ORDER[1])
        overwrite(first)
        rest_q.extend(quantize_weight("w1_rest%d" % a, w1_rest[a], placed("w1_rest_codes%d" % a, [P, H - SUB], U32, 52 + 1.5 * a)) for a in range(PASSES))
        w3_raw = load_weight("w3_raw", w3, 0)
        w3_grouped = group_weight("w3", w3_raw, slice(0, PACK), False, 48)
        load_factor(SLOT_ORDER[3])
        lift_col = load_per_row("lift_col", lift, 44)
        w4_codes = placed("w4_codes", [P, 2 * N], U8, 44.5)
        nc.sync.dma_start(out=w4_codes[:].bitcast(I32), in_=w4_words[0].bitcast(I32))
        w4_plane = placed("w4_plane", [P, 1, N], U8, 45)
        nc.gpsimd.memset(w4_plane[:].bitcast(I32), 0)
        load_scale_rows(nc.sync, w4_plane, w4_scales)

        for t in SLOT_ORDER[1:]:
            products(t)
        fetch_opponent(first)
        fetch_mover(first)
        nc.vector.tensor_scalar(mixed[first][:], opponent[first][:], mix_col[:, first : first + 1], None, ALU.mult)
        readings(SLOT_ORDER[1])
        for i, t in enumerate(SLOT_ORDER[:-1]):
            ahead = SLOT_ORDER[i + 1]
            overwrite(ahead)
            if i + 2 < PACK:
                readings(SLOT_ORDER[i + 2])
            else:
                w3_codes, w3_plane = quantize_weight("w3", w3_grouped, placed("w3_codes", [P, M], U32, 40))
            compare(t)
            if i + 2 < PACK:
                load_page(SLOT_ORDER[i + 2])
            fetch_opponent(ahead)
            put_opponent(t)
            fetch_mover(ahead)
            put_mover(t)
            if i == 0:
                spent = ["w1_rest0_plane"] + ["v_codes%d%d" % (a, h) for a in range(PASSES) for h in range(2)]
                spent = spent + ["second%d%d" % (u, h) for u in SLOT_ORDER[2:] for h in range(2)]
                woven.extend(
                    keep.tile([P, WIDTHS[c], PACK], BF16, name="woven%d" % c, tag=spent[c], align_bytes=64)
                    for c in range(CHUNKS)
                )
            for c in range(CHUNKS):
                weave(t, c, False)
        compare(last)
        put_mover(last)
        put_opponent(last)

        out_rows = out.rearrange("(j p) c -> p j c", p=P)
        for c in range(VECTOR_ROUNDED_CHUNKS, CHUNKS):
            weave(last, c, False)
        for c in range(CHUNKS):
            width = WIDTHS[c]
            if c < VECTOR_ROUNDED_CHUNKS:
                weave(last, c, True)
            b_codes = work.tile([P, width], U32, name="b_codes", bufs=CHUNKS, align_bytes=64)
            b_plane = work.tile([P, width], U8, name="b_plane", bufs=CHUNKS, align_bytes=64)
            nc.vector.quantize_mx(
                out=b_codes[:].bitcast(FP8X4), scales=b_plane[:], in_=woven[c][:].rearrange("p n t -> p (n t)")
            )
            y = work.tile([P, width, PACK], F32, name="y", bufs=3)
            for s in range(width // SUB):
                cols = slice(s * SUB, (s + 1) * SUB)
                sums = psum.tile([P, PACK, SUB], F32, name="sums", tag="bank%d" % ((STARTS[c] // SUB + s) % 5))
                for t in range(PACK):
                    rows = slice(t * SUB, (t + 1) * SUB)
                    nc.tensor.matmul_mx(
                        out=sums[:, t, :], lhsT=w3_codes[:, rows].bitcast(FP8X4), lhsT_scale=w3_plane[:, rows],
                        rhs=b_codes[:, cols].bitcast(FP8X4), rhs_scale=b_plane[:, cols], start=True, stop=True,
                    )
                nc.scalar.activation(out=y[:, cols, :], in_=sums[:].rearrange("p t n -> p n t"), func=ACT.Tanh)
            z = work.tile([P, width, PACK], BF16, name="z", bufs=3, align_bytes=64)
            nc.vector.tensor_tensor(
                out=z[:], in0=y[:], in1=lift_col[:].unsqueeze(1).to_broadcast([P, width, PACK]), op=ALU.mult
            )
            z_codes = work.tile([P, width], U32, name="z_codes", bufs=3, align_bytes=64)
            z_plane = work.tile([P, width], U8, name="z_plane", bufs=3, align_bytes=64)
            nc.vector.quantize_mx(
                out=z_codes[:].bitcast(FP8X4), scales=z_plane[:], in_=z[:].rearrange("p n t -> p (n t)")
            )
            scores = psum.tile([P, N // P, width], F32, name="scores", tag="bank%d" % (5 + c % 3))
            for j in range(N // P):
                nc.tensor.matmul_mx(
                    out=scores[:, j, :], lhsT=w4_codes[:, 2 * P * j : 2 * P * (j + 1)].bitcast(FP4X4),
                    lhsT_scale=w4_plane[:, 0, P * j : P * (j + 1)],
                    rhs=z_codes[:].bitcast(FP8X4), rhs_scale=z_plane[:], start=True, stop=True,
                )
            staged = work.tile([P, N // P, width], F32, name="staged", bufs=4)
            nc.scalar.copy(out=staged[:], in_=scores[:])
            nc.sync.dma_start(out=out_rows[:, :, STARTS[c] : STARTS[c] + width], in_=staged[:])
